import numpy as np
import ml_dtypes

BF16 = ml_dtypes.bfloat16


def bf(x):
    return np.asarray(x, np.float32).astype(BF16)


def f32(x):
    return np.asarray(x, np.float32)


def f64(x):
    return np.asarray(x).astype(np.float64)


def striped(idx):
    return np.tile(idx.reshape(-1, 16).T, (8, 1))


def rows(idx, k):
    return np.tile(idx, (k, 1))


def look(tab, idx):
    return np.take_along_axis(f64(tab), rows(idx, len(tab)), axis=1)


K, S, V, N = 256, 2048, 512, 512


def angles():
    a = np.random.uniform(0.0, 2.0 * np.pi, (K, S))
    return np.stack([np.cos(a), np.sin(a)])


def setup_inputs():
    return {"tab": bf(angles()), "x0": bf(np.random.standard_normal((K, V))), "x1": bf(np.random.standard_normal((K, V))), "offs": striped(np.random.randint(0, S, N))}


def reference(tab, x0, x1, offs):
    idx = offs[:16].T.reshape(-1)
    x = f64(x0) * look(tab[0], idx) + f64(x1) * look(tab[1], idx)
    return x

@@ -1,0 +1,28 @@
+import concourse.mybir as mybir
+
+BF16, F32, U16 = mybir.dt.bfloat16, mybir.dt.float32, mybir.dt.uint16
+MULT, ADD = mybir.AluOpType.mult, mybir.AluOpType.add
+P = 128
+
+
+def tile_lookup_rope_mul_out_kernel(tc, tab, x0, x1, offs, out):
+    nc = tc.nc
+    positions = tab.shape[2]
+    rows, picks = x0.shape
+    with tc.tile_pool(name="held", bufs=1) as held:
+        offsets = held.tile(list(offs.shape), U16, name="offsets")
+        nc.sync.dma_start(offsets[:], offs)
+        for block in range(rows // P):
+            block_rows = slice(block * P, (block + 1) * P)
+            products = []
+            for part, values_dram in enumerate((x0, x1)):
+                values = held.tile([P, picks], BF16, name=f"values{block}{part}")
+                window = held.tile([P, positions], BF16, name=f"window{block}{part}")
+                product = held.tile([P, picks], BF16, name=f"product{block}{part}")
+                nc.sync.dma_start(values[:], values_dram[block_rows, :])
+                nc.sync.dma_start(window[:], tab[part, block_rows, :])
+                nc.vector.tensor_tensor(product[:], window[:].indirect(offsets[:]), values[:], MULT)
+                products.append(product)
+            rotated = held.tile([P, picks], F32, name=f"rotated{block}")
+            nc.vector.tensor_tensor(rotated[:], products[0][:], products[1][:], ADD)
+            nc.scalar.dma_start(out[block_rows, :], rotated[:])

@@ -9,20 +9,29 @@ def tile_lookup_rope_mul_out_kernel(tc, tab, x0, x1, offs, out):
     nc = tc.nc
     positions = tab.shape[2]
     rows, picks = x0.shape
+    half = picks // 2
     with tc.tile_pool(name="held", bufs=1) as held:
         offsets = held.tile(list(offs.shape), U16, name="offsets")
-        nc.sync.dma_start(offsets[:], offs)
+        windows, values = {}, {}
+        for block in range(rows // P):
+            block_rows = slice(block * P, (block + 1) * P)
+            for part, values_dram in enumerate((x0, x1)):
+                windows[block, part] = held.tile([P, positions], BF16, name=f"window{block}{part}")
+                values[block, part] = held.tile([P, picks], BF16, name=f"values{block}{part}")
+                nc.sync.dma_start(windows[block, part][:], tab[part, block_rows, :])
+                if (block, part) == (0, 0):
+                    nc.sync.dma_start(offsets[:], offs)
+                nc.sync.dma_start(values[block, part][:], values_dram[block_rows, :])
         for block in range(rows // P):
             block_rows = slice(block * P, (block + 1) * P)
             products = []
-            for part, values_dram in enumerate((x0, x1)):
-                values = held.tile([P, picks], BF16, name=f"values{block}{part}")
-                window = held.tile([P, positions], BF16, name=f"window{block}{part}")
+            for part in range(2):
                 product = held.tile([P, picks], BF16, name=f"product{block}{part}")
-                nc.sync.dma_start(values[:], values_dram[block_rows, :])
-                nc.sync.dma_start(window[:], tab[part, block_rows, :])
-                nc.vector.tensor_tensor(product[:], window[:].indirect(offsets[:]), values[:], MULT)
+                looked_up = windows[block, part][:].indirect(offsets[:])
+                nc.vector.tensor_tensor(product[:], looked_up, values[block, part][:], MULT)
                 products.append(product)
-            rotated = held.tile([P, picks], F32, name=f"rotated{block}")
-            nc.vector.tensor_tensor(rotated[:], products[0][:], products[1][:], ADD)
-            nc.scalar.dma_start(out[block_rows, :], rotated[:])
+            for side, queue in enumerate((nc.scalar, nc.sync)):
+                columns = slice(side * half, (side + 1) * half)
+                rotated = held.tile([P, half], F32, name=f"rotated{block}{side}")
+                nc.vector.tensor_tensor(rotated[:], products[0][:, columns], products[1][:, columns], ADD)
+                queue.dma_start(out[block_rows, columns], rotated[:])

@@ -1,4 +1,5 @@
 import concourse.mybir as mybir
+from concourse.masks import make_identity
 
 BF16, F32, U16 = mybir.dt.bfloat16, mybir.dt.float32, mybir.dt.uint16
 MULT, ADD = mybir.AluOpType.mult, mybir.AluOpType.add
@@ -9,11 +10,12 @@ def tile_lookup_rope_mul_out_kernel(tc, tab, x0, x1, offs, out):
     nc = tc.nc
     positions = tab.shape[2]
     rows, picks = x0.shape
+    blocks = rows // P
     half = picks // 2
-    with tc.tile_pool(name="held", bufs=1) as held:
+    with tc.tile_pool(name="held", bufs=1) as held, tc.psum_pool(name="psum", bufs=1) as psum:
         offsets = held.tile(list(offs.shape), U16, name="offsets")
         windows, values = {}, {}
-        for block in range(rows // P):
+        for block in range(blocks):
             block_rows = slice(block * P, (block + 1) * P)
             for part, values_dram in enumerate((x0, x1)):
                 windows[block, part] = held.tile([P, positions], BF16, name=f"window{block}{part}")
@@ -22,7 +24,9 @@ def tile_lookup_rope_mul_out_kernel(tc, tab, x0, x1, offs, out):
                 if (block, part) == (0, 0):
                     nc.sync.dma_start(offsets[:], offs)
                 nc.sync.dma_start(values[block, part][:], values_dram[block_rows, :])
-        for block in range(rows // P):
+        identity = held.tile([P, P], BF16, name="identity")
+        make_identity(nc, identity[:])
+        for block in range(blocks):
             block_rows = slice(block * P, (block + 1) * P)
             products = []
             for part in range(2):
@@ -30,8 +34,16 @@ def tile_lookup_rope_mul_out_kernel(tc, tab, x0, x1, offs, out):
                 looked_up = windows[block, part][:].indirect(offsets[:])
                 nc.vector.tensor_tensor(product[:], looked_up, values[block, part][:], MULT)
                 products.append(product)
-            for side, queue in enumerate((nc.scalar, nc.sync)):
-                columns = slice(side * half, (side + 1) * half)
-                rotated = held.tile([P, half], F32, name=f"rotated{block}{side}")
-                nc.vector.tensor_tensor(rotated[:], products[0][:, columns], products[1][:, columns], ADD)
-                queue.dma_start(out[block_rows, columns], rotated[:])
+            if block < blocks - 1:
+                summed = psum.tile([P, picks], F32, name=f"summed{block}")
+                nc.tensor.matmul(summed[:], identity[:], products[0][:], start=True, stop=False)
+                nc.tensor.matmul(summed[:], identity[:], products[1][:], start=False, stop=True)
+                rotated = held.tile([P, picks], F32, name=f"rotated{block}")
+                nc.scalar.copy(rotated[:], summed[:])
+                nc.sync.dma_start(out[block_rows, :], rotated[:])
+            else:
+                for side in range(2):
+                    columns = slice(side * half, (side + 1) * half)
+                    rotated = held.tile([P, half], F32, name=f"rotated{block}{side}")
+                    nc.vector.tensor_tensor(rotated[:], products[0][:, columns], products[1][:, columns], ADD)
+                    nc.sync.dma_start(out[block_rows, columns], rotated[:])

@@ -40,7 +40,7 @@ def tile_lookup_rope_mul_out_kernel(tc, tab, x0, x1, offs, out):
                 nc.tensor.matmul(summed[:], identity[:], products[1][:], start=False, stop=True)
                 rotated = held.tile([P, picks], F32, name=f"rotated{block}")
                 nc.scalar.copy(rotated[:], summed[:])
-                nc.sync.dma_start(out[block_rows, :], rotated[:])
+                nc.scalar.dma_start(out[block_rows, :], rotated[:])
             else:
                 for side in range(2):
                     columns = slice(side * half, (side + 1) * half)

import concourse.mybir as mybir
from concourse.masks import make_identity

BF16, F32, U16 = mybir.dt.bfloat16, mybir.dt.float32, mybir.dt.uint16
MULT, ADD = mybir.AluOpType.mult, mybir.AluOpType.add
P = 128


def tile_lookup_rope_mul_out_kernel(tc, tab, x0, x1, offs, out):
    nc = tc.nc
    positions = tab.shape[2]
    rows, picks = x0.shape
    blocks = rows // P
    half = picks // 2
    with tc.tile_pool(name="held", bufs=1) as held, tc.psum_pool(name="psum", bufs=1) as psum:
        offsets = held.tile(list(offs.shape), U16, name="offsets")
        windows, values = {}, {}
        for block in range(blocks):
            block_rows = slice(block * P, (block + 1) * P)
            for part, values_dram in enumerate((x0, x1)):
                windows[block, part] = held.tile([P, positions], BF16, name=f"window{block}{part}")
                values[block, part] = held.tile([P, picks], BF16, name=f"values{block}{part}")
                nc.sync.dma_start(windows[block, part][:], tab[part, block_rows, :])
                if (block, part) == (0, 0):
                    nc.sync.dma_start(offsets[:], offs)
                nc.sync.dma_start(values[block, part][:], values_dram[block_rows, :])
        identity = held.tile([P, P], BF16, name="identity")
        make_identity(nc, identity[:])
        for block in range(blocks):
            block_rows = slice(block * P, (block + 1) * P)
            products = []
            for part in range(2):
                product = held.tile([P, picks], BF16, name=f"product{block}{part}")
                looked_up = windows[block, part][:].indirect(offsets[:])
                nc.vector.tensor_tensor(product[:], looked_up, values[block, part][:], MULT)
                products.append(product)
            if block < blocks - 1:
                summed = psum.tile([P, picks], F32, name=f"summed{block}")
                nc.tensor.matmul(summed[:], identity[:], products[0][:], start=True, stop=False)
                nc.tensor.matmul(summed[:], identity[:], products[1][:], start=False, stop=True)
                rotated = held.tile([P, picks], F32, name=f"rotated{block}")
                nc.scalar.copy(rotated[:], summed[:])
                nc.scalar.dma_start(out[block_rows, :], rotated[:])
            else:
                for side in range(2):
                    columns = slice(side * half, (side + 1) * half)
                    rotated = held.tile([P, half], F32, name=f"rotated{block}{side}")
                    nc.vector.tensor_tensor(rotated[:], products[0][:, columns], products[1][:, columns], ADD)
                    nc.sync.dma_start(out[block_rows, columns], rotated[:])
